import numpy as np, ml_dtypes
CORES = [2,3,42,43,82,83,122,123]
N = 8
import mx_ref
BF = ml_dtypes.bfloat16
def gentries(a):
    return np.ascontiguousarray(a.reshape(8, 16, -1).transpose(0, 2, 1)).reshape(8, -1)
def gtable(e):
    e = np.asarray(e); return np.ascontiguousarray(e.reshape(8, -1, 16).transpose(0, 2, 1)).reshape(128, -1).astype(np.int32)
def gcols(t, e):
    v = np.concatenate([t.reshape(8, 16, -1, 4), np.zeros((8, 16, 1, 4), BF)], axis=2)
    return np.ascontiguousarray(np.stack([v[g][:, e[g]] for g in range(8)])).reshape(128, -1)
def tile(rs):
    return np.stack(rs, axis=2).reshape(128, -1).astype(BF)
def pick(q, e):
    c = np.concatenate([q[0].reshape(128, -1, 4), np.zeros((128, 1, 4), np.uint8)], axis=1); s = np.concatenate([q[1], np.ones((16, 1), np.uint8)], axis=1)
    return (np.ascontiguousarray(c[:, e].reshape(128, -1)), np.ascontiguousarray(s[:, e]))
def join(*qs):
    return (np.concatenate([q[0] for q in qs], axis=1), np.concatenate([q[1] for q in qs], axis=1))
def put(q, e, v):
    c, s = q[0].reshape(128, -1, 4).copy(), q[1].copy(); c[:, e] = v[0].reshape(128, -1, 4); s[:, e] = v[1]
    return (c.reshape(128, -1), s)
def pk(c, s):
    return (np.ascontiguousarray(c), mx_ref.live(s))
def emit(q):
    return q[0], q[1]
def packed(v, rng):
    q = [mx_ref.quantize(np.ascontiguousarray(v[r])) for r in range(N)]
    return np.stack([a for a, b in q]), np.stack([mx_ref.plane(b, rng) for a, b in q])
def values_of_codes():
    e, c = np.zeros((128, 128, 4), np.float32), np.zeros((128, 2, 4), np.uint8)
    e[np.arange(128), np.arange(128), 0] = 1
    c[:127, :, 0] = np.arange(256).reshape(2, 128).T[:127]
    return mx_ref.matmul(mx_ref.quantize(e.reshape(128, 512).astype(BF)), (c.reshape(128, 8), np.full((16, 2), 127, np.uint8))).T.reshape(-1).astype(np.float64)
CODE_VALUE, SCALE_VALUE = values_of_codes(), 2.0 ** (np.arange(256) - 127.0)
def decode(q):
    return (CODE_VALUE[q[0]].reshape(16, 8, -1, 4) * SCALE_VALUE[q[1]][:, None, :, None] + 0.0).reshape(128, -1).astype(np.float32)
def f(rng, *shape):
    return mx_ref.flush((rng.standard_normal(shape, dtype=np.float32) * np.exp2(rng.integers(-2, 3, shape[:-1] + (1,)))).astype(BF))
def wide(rng, *shape, cols=0):
    v = rng.standard_normal(shape, dtype=np.float32) * np.exp2(rng.integers(-12, 13, shape)).astype(np.float32)
    if cols: v *= np.repeat(np.exp2(rng.integers(-cols, cols + 1, shape[:-2] + (1, shape[-1] // 4))) * (rng.random(shape[:-2] + (1, shape[-1] // 4)) > 0.0625), 4, axis=-1).astype(np.float32)
    return mx_ref.flush(v.astype(BF))
C, K, R = 256, 56, 3
def rings(o):
    e = np.zeros((N, 8, C), int)
    np.put_along_axis(e, o, np.roll(o, -1, axis=2), axis=2)
    return np.stack([gtable(e[r]) for r in range(N)])
def orders(rng):
    return np.argsort(rng.random((N, 8, C)), axis=2)
def numbers_of(rng):
    return {"x": np.array(f(rng, N, 128, 4 * C)), "u": np.array(f(rng, N, 128, 512)), "v": np.array(f(rng, N, 128, 512))}
def layers(rng):
    return np.array(f(rng, N, 128, 2048)).reshape(N, 8, 16, 4, 8, 16, 4)
def carry(source, size):
    w = np.zeros((N, 128, 4, 128, 4), np.float32)
    i = np.arange(128)
    for b in range(4): w[:, i - i % 16 + np.array(source)[i % 16], b, i, b] = 32 * np.resize(size, 128)
    return w.astype(BF)
def weights(rng, w):
    c, p = packed(np.ascontiguousarray(w).reshape(N, 128, 2048), rng)
    return {"wc": c, "ws": p}
def signs(rng):
    return np.stack([rng.permutation(8) % 2 * 2.0 - 1.0 for r in range(N)])
def setup_inputs(rng):
    return {**numbers_of(rng), **weights(rng, layers(rng)), "nx": rings(orders(rng))}
def setup_inputs_ties(rng):
    d = numbers_of(rng)
    x = d["x"].astype(np.float32).reshape(N, 8, 16, C, 4)
    e = (rng.integers(N) + np.arange(N)) % N
    w = layers(rng)
    o = orders(rng)
    for i in range(N):
        r = e[i]
        k = np.stack([rng.permutation(C) % 3 - 1 for g in range(8)])
        if i < 2: k[:] = i
        x[r][:, :8] = np.abs(x[r][:, :8, :1]) * k[:, None, :, None]
        if i >= 3 and i % 2 == 1: w[r][:, :, :, :, :8] = 0
        g = rng.permutation(8)
        o[r, g[0]] = np.arange(C)
        o[r, g[1]] = np.arange(C)[::-1]
    u = d["u"].astype(np.float32).reshape(N, 8, 16, 8, 16, 4)
    k = np.abs(u)
    u[:, :, :, :, 0] = 0
    for g in range(8): u[:, g, :8, g, 0] = k[:, g, :8, g, 0]
    return {"x": x.reshape(N, 128, 4 * C).astype(BF), "u": u.reshape(N, 128, 512).astype(BF), "v": d["v"], **weights(rng, w), "nx": rings(o)}
def setup_inputs_near(rng):
    d = numbers_of(rng)
    x = d["x"].astype(np.float32).reshape(N, 8, 16, C, 4)
    x[:, :, :2] = 0
    u = d["u"].reshape(N, 128, 128, 4)
    u[:, :, ::16] = 0
    e = rng.permutation(8)
    for g in range(8):
        if e[g] < 4:
            s, size, k = rng.integers(-2, 3, (N, 2, C)), 2.0 ** -30, 2.0 ** -30
        else:
            s, size, k = rng.integers(0, 16, (N, 2, C)), 2.0 ** -23, 1.0
            x[:, g, 0, :, 0] = rng.choice([-1.0, 1.0], (N, C))
            x[:, g, 1, :, 0] = e[g] % 2 * 2.0 - 1.0
        x[:, g, 8:10] = ((np.abs(s)[..., None] >> np.arange(4)) & 1) * np.sign(s)[..., None] * np.exp2(np.arange(4.0)) * size
        x[:, g, 10:] = rng.integers(4, 8, (N, 6, C, 4)) * 2 * size
        u[:, 16 * g, 16 * g, 0] = k
        u[:, 16 * g + 8, 16 * g] = k
    times = np.resize(np.array([1.0, 1.0] + [0.75] * 6 + [1.0, 1.0] + [0.75] * 6), (8, 16))
    times[e < 4, 8:10] = 2.0 ** -7
    w = carry([1, 1, 2, 3, 4, 5, 6, 7, 9, 8, 10, 11, 12, 13, 14, 15], times)
    return {"x": x.reshape(N, 128, 4 * C).astype(BF), "u": u.reshape(N, 128, 512), "v": d["v"], **weights(rng, w), "nx": rings(orders(rng))}
def setup_inputs_huge(rng):
    d = numbers_of(rng)
    x = 2.0 ** 30 * (0.8 + 0.2 * rng.random((N, 8, 16, C, 4)))
    for r in range(N): x[r, :, :8] *= (rng.permutation(C) % 2 * 2.0 - 1.0)[:, None]
    u = d["u"].reshape(N, 8, 16, 8, 16, 4)
    u[:, :, :, :, 0] = 0
    a = 2.0 ** 30 * (0.8 + 0.2 * rng.random((N, 8, 8, 8, 4))) * signs(rng)[:, None, None, :, None]
    u[:, :, :8, :, 0] = a.astype(np.float32).astype(BF)
    w = carry([8, 9, 10, 11, 12, 13, 14, 15, 0, 1, 2, 3, 4, 5, 6, 7], [0.875] * 16)
    o = np.zeros((N, 8, C), int) + rng.permutation(C)
    return {"x": x.astype(np.float32).reshape(N, 128, 4 * C).astype(BF), "u": u.reshape(N, 128, 512), "v": d["v"], **weights(rng, w), "nx": rings(o)}
def setup_inputs_slots(rng):
    d = numbers_of(rng)
    n = [0, 1, C // 2, K + 1, K, K - 1, K, K + 1]
    e = rng.permutation(8)
    o = orders(rng)
    x = d["x"].astype(np.float32).reshape(N, 8, 16, C, 4)
    for r in range(N):
        for g in range(8):
            turns = np.sort(rng.permutation(C)[:2 * n[(e[g] + r) % 8]])
            s = (np.searchsorted(turns, np.arange(C), side="right") + rng.integers(2)) % 2
            x[r, g, 0][o[r, g], 0] = 2.0 * s - 1.0
    u = d["u"].reshape(N, 128, 128, 4)
    u[:, :, ::16] = 0
    for h in range(0, 128, 16): u[:, h, h, 0] = 1
    return {"x": x.reshape(N, 128, 4 * C).astype(BF), "u": u.reshape(N, 128, 512), "v": d["v"], **weights(rng, layers(rng)), "nx": rings(o)}
def setup_inputs_spread(rng):
    d = setup_inputs(rng)
    d["x"] = wide(rng, N, 128, 4 * C, cols=6)
    return d
def check_inputs(d):
    b = []
    for k in ("x", "u", "v"):
        a = np.abs(d[k].astype(np.float32))
        if not (np.isfinite(a).all() and ((a == 0) | (a >= 2.0 ** -30) & (a <= 2.0 ** 30)).all()): b.append("a value of " + k)
    if ((d["wc"] & 0x7F) == 0x7F).any(): b.append("a code of wc that is no number")
    z = np.zeros((128, 4, 4), np.float32)
    z[:, 1] = 2.0 ** -30
    z[:, 2] = 2.0 ** 30
    c, s = emit(mx_ref.quantize(z.reshape(128, 16).astype(BF)))
    for r in range(N):
        p = mx_ref.live(d["ws"][r])
        if not ((p == s[0, 0]) | (p >= s[0, 1]) & (p <= s[0, 2])).all(): b.append("a scale of ws")
        e = gentries(d["nx"][r])
        good = bool(((e >= 0) & (e < C)).all())
        j = np.zeros(8, int)
        for i in range(C):
            if good:
                j = e[np.arange(8), j]
                good = bool(((j == 0) == (i == C - 1)).all())
        if not good: b.append("a ring of nx")
    return b
def reference(x, u, v, wc, ws, nx):
    qu = [mx_ref.quantize(u[r]) for r in range(N)]
    lay = [pk(wc[r], ws[r]) for r in range(N)]
    after = [gentries(nx[r]) for r in range(N)]
    before = [np.argsort(after[r], axis=1) for r in range(N)]
    now = [x[r] for r in range(N)]
    for t in range(R):
        forward, parts, sent, count = [], [], [], []
        for r in range(N):
            q = mx_ref.quantize(now[r])
            a = mx_ref.matmul(qu[r], q)[::16] > 0
            p = decode(q).astype(BF)
            e, n = np.full((8, 2 * K), -1), np.zeros(8, int)
            for g in range(8):
                j = np.flatnonzero(a[g] & ~a[g][after[r][g]])[:K]
                n[g] = len(j)
                e[g, 0:2 * len(j):2] = j
                e[g, 1:2 * len(j):2] = after[r][g][j]
            forward.append(a)
            parts.append(p)
            sent.append(mx_ref.quantize(gcols(p, e)))
            count.append(n)
        made, lists = [], []
        for r in range(N):
            z, n = sent[r - 1], count[r - 1]
            h = tile([mx_ref.matmul(pick(lay[r], np.arange(128 * b, 128 * b + 128)), z) * np.float32(0.03125) for b in range(4)])
            p = mx_ref.matmul(qu[r], mx_ref.quantize(h))[::16]
            swap = (p[:, 1::2] > p[:, 0::2]).astype(int)
            e = np.where(forward[r], before[r], after[r])
            for g in range(8):
                a, o = forward[r][g], after[r][g]
                j = np.flatnonzero(~a & a[o])
                e[g, j] = j
                e[g, o[j]] = o[j]
                j = j[:n[g]]
                k = np.arange(len(j))
                e[g, j] = C + 2 * k + swap[g, k]
                e[g, o[j]] = C + 2 * k + 1 - swap[g, k]
            made.append(gcols(np.concatenate([parts[r], h], axis=1), e))
            lists.append(e)
        now = made
    y, ot = np.zeros((N, 128, C), np.float32), np.zeros((N, 8, C), np.float32)
    oc, osc = np.zeros((N, 128, 4 * C), np.uint8), np.zeros((N, 16, C), np.uint8)
    for r in range(N):
        q = mx_ref.quantize(now[r])
        y[r] = mx_ref.matmul(mx_ref.quantize(v[r]), q)
        ot[r] = lists[r]
        oc[r], osc[r] = emit(q)
    return {"y": y, "ot": ot, "oc": oc, "osc": osc}

@@ -1,0 +1,347 @@
+from concourse.mybir import dt, AluOpType as A, ActivationFunctionType as F
+
+R, C, K = 3, 256, 56
+PW = 384
+H0 = 272
+LW = 2 * K
+BIG = float(2 ** 24)
+SKIP = 24
+X4, U8, BF, F32, I32, U16 = "float8_e4m3fn_x4", "uint8", "bfloat16", "float32", "int32", "uint16"
+
+SCRATCH = {"ps": ("psum", [128, 1024], F32), "pd": ("psum", [128, 2048], F32), "pp": ("psum", [128, 512], F32)}
+for _d, _l in (
+    (BF, "xin 1024 uin 512 vin 512 ze 528 nl 32 th 1536 at 512 ht 512 j32 32 jrow 256 thr 8 ka 32 kb 32 kx 256 "
+         "nxrow 272 pvrow 256 pvs 256 fl 256 sg 256 mt 256 cum 768 cmp 512 cs 256 sgn 512 nval 80 nsc 64 hh 272 "
+         "zz 256 zp 256 cv 768 gt 384 dv 256 ds 256 xs0 1024 xs1 1024 xs2 1024"),
+    (X4, "wq 512 qu 128 qur 128 qv 128 qe 512 lq 464 qx0 256 qx1 256 qx2 256 qx3 256 qa0 128 qa1 128 qa2 128 "
+         "qh0 128 qh1 128 qh2 128"),
+    (U8, "wsc 512 su 128 sur 128 sv 128 se 512 ls 464 sx0 256 sx1 256 sx2 256 sx3 256 sa0 128 sa1 128 sa2 128 "
+         "sh0 128 sh1 128 sh2 128"),
+    (I32, "nxi 16 i1 128 i3 16 ip 16 pm 16 ui 64 odd 64 kf 32"),
+    (U16, "uoff 8 nx16 16 pv16 16 offa 8 kk16 16 offx 16"),
+    (F32, "spec 384 col 16 jw 16 jq 16 thb 8 pvf 16 dp0 16 acc 8 pa 64 cc 32 jn 16 dpn 16 nm2 8 ww 32 "
+          "vw 32 ta 16 tb 16 nsp 16 tc 16 td 16 te 16 kk 16 tv 16 kr 16 base 16 fin 16 otr 256 ysb 256"),
+):
+    _w = _l.split()
+    for _i in range(0, len(_w), 2):
+        SCRATCH[_w[_i]] = ("sbuf", [128, int(_w[_i + 1])], _d)
+
+SEMAPHORES = (["cv_", "cs_", "ct_", "cg_"] + ["d%d" % i for i in range(16)]
+              + ["%s%d" % (n, r) for n in ("arn", "ara", "lon", "loa") for r in range(R)])
+
+
+def rank_program(g, core, T, topo):
+    rank = T.rank_of(core)
+    if rank is None:
+        return
+    cores = list(T.cores)
+    nxt, prv = cores[(rank + 1) % len(cores)], cores[rank - 1]
+    rid, pid = topo.addr(nxt)[:2]
+    out_mask, n_out, n_in = topo.mask(core, nxt), len(topo.engines(core, nxt)), len(topo.engines(prv, core))
+
+    Q = {"v": g.vector, "s": g.scalar, "t": g.tensor, "g": g, "y": g.sync}
+    own = {"v": "cv_", "s": "cs_", "t": "ct_", "g": "cg_"}
+    total = {}
+    known = {e: {} for e in Q}
+    wrote, read = {}, {}
+    ndma = [0]
+
+    def need(e, ev):
+        sem, cnt, clock = ev[1], ev[2], ev[3]
+        if known[e].get(sem, 0) >= cnt:
+            return
+        Q[e].wait_ge(T.sem[sem], cnt)
+        known[e][sem] = cnt
+        for k, c in clock.items():
+            if known[e].get(k, 0) < c:
+                known[e][k] = c
+
+    def deps(e, reads, writes):
+        evs = []
+        for k in reads.split():
+            if k in wrote:
+                evs.append(wrote[k])
+            if k[0] == "P":
+                evs += [x for x in read.get(k, []) if x[0] != e]
+        for k in writes.split():
+            if k in wrote:
+                evs.append(wrote[k])
+            evs += read.get(k, [])
+        for ev in sorted(evs, key=lambda x: -x[2]):
+            need(e, ev)
+
+    def note(ev, reads, writes):
+        for k in reads.split():
+            read.setdefault(k, []).append(ev)
+        for k in writes.split():
+            wrote[k] = ev
+            read[k] = []
+
+    def op(e, fn, reads, writes):
+        deps(e, reads, writes)
+        sem = own[e]
+        total[sem] = total.get(sem, 0) + 1
+        fn().then_inc(T.sem[sem], 1)
+        note((e, sem, total[sem], dict(known[e])), reads, writes)
+
+    def dma(e, out, in_, reads, writes):
+        deps(e, reads, writes)
+        sem = "d%d" % ndma[0]
+        ndma[0] += 1
+        total[sem] = 16
+        Q[e].dma_start(out, in_).then_inc(T.sem[sem], 16)
+        note(("dma", sem, 16, dict(known[e])), reads, writes)
+
+    def send(out, in_, reads, rsem, lsem):
+        deps("g", reads, "")
+        g.remote_dma(out, in_, T.sem[rsem], T.sem[lsem], pid, rid, out_mask)
+        total[lsem] = total.get(lsem, 0) + n_out
+
+    V, S, PE = g.vector, g.scalar, g.tensor
+
+    def ts(out, in0, s1, o0, reads, writes, s2=None, o1=None):
+        if o1 is None:
+            op("v", lambda: V.tensor_scalar(out, in0, s1, None, o0), reads, writes)
+        else:
+            op("v", lambda: V.tensor_scalar(out, in0, s1, s2, o0, o1), reads, writes)
+
+    def tt(out, a, b, o, reads, writes):
+        op("v", lambda: V.tensor_tensor(out, a, b, o), reads, writes)
+
+    def cp(out, in_, reads, writes):
+        op("v", lambda: V.tensor_copy(out, in_), reads, writes)
+
+    def scan(out, d0, d1, o0, o1, reads, writes):
+        op("v", lambda: V.tensor_tensor_scan(out, d0, d1, 0.0, o0, o1), reads, writes)
+
+    def hold(out, row, n, reads, writes):
+        scan(out, T.kx[:, 0:n], row, A.mult, A.add, reads + " kx", writes)
+
+    def quant(q, s, in_, reads, writes):
+        op("v", lambda: V.quantize_mx(q, s, in_), reads, writes)
+
+    def act(out, in_, reads, writes, scale=None, func=F.Copy):
+        if scale is not None:
+            op("s", lambda: S.activation(out, in_, func, scale=scale), reads, writes)
+        else:
+            op("s", lambda: S.activation(out, in_, func), reads, writes)
+
+    def count(out, in_, bias, acc, reads, writes):
+        op("s", lambda: S.activation(out, in_, F.Sign, bias=bias, scale=-1.0, accum_out=acc), reads, writes)
+
+    def mm(out, w, ws, x, xs, reads, writes):
+        op("t", lambda: PE.matmul_mx(out, w, ws, x, xs, True, True), reads, writes)
+
+    def iota(out, pat, base, cm, key, small=False):
+        if small:
+            op("g", lambda: g.iota(out, pat, base, cm, allow_small_or_imprecise_dtypes=True), "", key)
+        else:
+            op("g", lambda: g.iota(out, pat, base, cm), "", key)
+
+    for r in range(R):
+        total["arn%d" % r] = n_in
+        total["ara%d" % r] = 2 * n_in
+        wrote["nl%d" % r] = ("net", "arn%d" % r, n_in, {})
+        wrote["land%d" % r] = ("net", "ara%d" % r, 2 * n_in, {})
+
+    HK = "h0 h1 h2 h3"
+    PM, PM1, INV, SC, RSC, NW = [T.col[:, i:i + 1] for i in range(6)]
+
+    dma("s", T.nxi[:], T.nx[:], "", "nxi")
+    dma("y", T.uin[:], T.u[:], "", "uin")
+    dma("s", T.xin[:, 0:512], T.x[:, 0:512], "", "xin0")
+    dma("y", T.xin[:, 512:1024], T.x[:, 512:1024], "", "xin1")
+    deps("y", "uin xin0 xin1", "")
+    dma("y", T.wq[:].bitcast(dt.uint8), T.wc[:], "", "wq")
+    dma("y", T.wsc[:], T.ws[:], "", "wsc")
+    dma("y", T.vin[:], T.v[:], "", "vin")
+
+    iota(T.i1[:], [[1, 128]], 0, -1, "i1")
+    iota(T.ip[:], [[0, 16]], 0, 1, "ip")
+    iota(T.i3[:], [[16, 16]], 0, 0, "i3")
+    iota(T.jrow[:], [[1, 256]], 0, 0, "jrow", True)
+    iota(T.j32[:], [[0, 2], [1, 16]], 0, 0, "j32", True)
+    iota(T.spec[:, 0:H0], [[1, H0]], 0, 0, "spec0", True)
+    iota(T.spec[:, H0:PW], [[1, 2], [2, K]], C, 0, "spec1", True)
+
+    op("v", lambda: V.memset(T.ze[:], 0.0), "", "ze")
+    op("v", lambda: V.memset(T.ht[:], 0.0), "", HK + " hpad")
+    op("v", lambda: V.memset(T.nxrow[:, 256:272], float(C)), "", "nxpad")
+    ts(T.ze[:, 3:515:4], T.i1[:], 0.0, A.is_equal, "i1", "ze")
+    ts(T.pm[:], T.ip[:], 15, A.bitwise_and, "ip", "pm")
+    cp(T.uoff[:], T.i3[:, 0:8], "i3", "uoff")
+    for b in range(4):
+        quant(T.qe[:, 128 * b:128 * b + 128], T.se[:, 128 * b:128 * b + 128], T.ze[:, 3 - b:515 - b], "ze", "e%d" % b)
+    tt(T.jw[:], T.pm[:], T.i3[:], A.add, "pm i3", "jw")
+    cp(PM, T.pm[:, 0:1], "pm", "pmf")
+    ts(PM1, T.pm[:, 0:1], 1.0, A.add, "pm", "pm1")
+    ts(INV, T.pm[:, 0:1], 15.0, A.is_equal, "pm", "inv", 1.0 / BIG, A.max)
+    ts(T.thr[:, 0:2], T.jw[:, 0:2], -8.0, A.add, "jw", "thr")
+    ts(T.thb[:, 0:2], T.jw[:, 2:4], -7.5, A.add, "jw", "thb")
+
+    for b in range(4):
+        act(T.th[:, PW * b + C:PW * b + H0], T.ht[:, 0:16], HK, "tz%d" % b)
+    act(T.nval[:, 64:80], T.ht[:, 0:16], HK, "nvpad")
+    act(T.hh[:, 0:16], T.ht[:, 0:16], HK, "hhpad")
+    act(T.gt[:, 0:H0], T.ht[:, 0:H0], HK, "g0")
+
+    cp(T.nx16[:], T.nxi[:], "nxi", "nx16")
+    ts(T.ka[:], T.j32[:], PM, A.not_equal, "j32 pmf", "ka")
+    ts(T.kb[:], T.j32[:], PM1, A.is_equal, "j32 pm1", "kb", BIG, A.mult)
+    act(T.nxrow[:, 0:256], T.jrow[:].indirect(T.nx16[:]), "jrow nx16", "nxrow")
+    tt(T.kx[:, 0:32], T.ka[:], T.kb[:], A.max, "ka kb", "kx0")
+    cp(T.pvrow[:].indirect(T.nx16[:]), T.jrow[:], "jrow nx16", "pvrow")
+    quant(T.qu[:], T.su[:], T.uin[:], "uin", "qu")
+    cp(T.qur[:].bitcast(dt.uint32), T.qu[:].bitcast(dt.uint32).indirect(T.uoff[:]), "qu uoff", "qur")
+    act(T.kx[:, 32:64], T.kx[:, 0:32], "kx0", "kx1")
+    act(T.kx[:, 64:128], T.kx[:, 0:64], "kx1", "kx2")
+    act(T.kx[:, 128:256], T.kx[:, 0:128], "kx2", "kx")
+    act(T.sur[:], T.su[:].indirect(T.uoff[:]), "qu uoff", "sur")
+
+    def quant_x(r):
+        src = T.xin if r == 0 else T["xs%d" % (r - 1)]
+        for h in range(2):
+            quant(T["qx%d" % r][:, 128 * h:128 * h + 128], T["sx%d" % r][:, 128 * h:128 * h + 128],
+                  src[:, 512 * h:512 * h + 512], "xin%d" % h if r == 0 else "x0 x1 x2 x3", "qx%d" % h)
+
+    for r in range(R):
+        qx, sx = T["qx%d" % r], T["sx%d" % r]
+        quant_x(r)
+        for h in range(2):
+            mm(T.ps[:, 512 * h:512 * h + 128], T.qur[:], T.sur[:], qx[:, 128 * h:128 * h + 128],
+               sx[:, 128 * h:128 * h + 128], "qur sur qx%d" % h, "PS%d" % h)
+        mm(T.pp[:, 0:128], T.qur[:], T.sur[:], qx[:, 128:256], sx[:, 128:256], "qur sur qx1", "PP")
+        for b in range(4):
+            mm(T.pd[:, 512 * b:512 * b + 256], T.qe[:, 128 * b:128 * b + 128], T.se[:, 128 * b:128 * b + 128],
+               qx[:], sx[:], "e%d qx0 qx1" % b, "PD%d" % b)
+
+        def unpack(b):
+            act(T.th[:, PW * b:PW * b + C], T.pd[:, 512 * b:512 * b + 256], "PD%d" % b, "t%d" % b)
+
+        act(T.sg[:, 0:128], T.ps[:, 0:128], "PS0", "sg0", func=F.Sign)
+        act(T.sg[:, 128:256], T.pp[:, 0:128], "PP", "sg1", func=F.Sign)
+        for h in (1, 0):
+            ts(T.fl[:, 128 * h:128 * h + 128], T.ps[:, 512 * h:512 * h + 128], 0.0, A.is_gt, "PS%d" % h, "fl%d" % h)
+        unpack(0)
+        unpack(1)
+        tt(T.mt[:], T.fl[:].indirect(T.nx16[:]), T.sg[:], A.is_lt, "fl0 fl1 sg0 sg1 nx16", "mt")
+        cum = T.cum[:, 256 * r:256 * r + 256]
+        ck = "cum%d" % r
+        scan(cum, T.mt[:], T.mt[:], A.add, A.max, "mt", ck)
+        send(T.nl[:, 8 * r:8 * r + 2], T.cum[:, 256 * r + 254:256 * r + 256], ck, "arn%d" % r, "lon%d" % r)
+        for c in range(2):
+            count(T.sgn[:, 256 * c:256 * c + C - SKIP], T.cum[:, 256 * r + SKIP:256 * r + 256], T.thb[:, c:c + 1],
+                  T.acc[:, c:c + 1], ck + " thb", "acc%d" % c)
+        unpack(2)
+        unpack(3)
+        for c in range(2):
+            ts(T.cmp[:, 256 * c:256 * c + 256], cum, T.thr[:, c:c + 1], A.is_le, ck + " thr", "cmp%d" % c)
+        for c in range(2):
+            scan(T.cs[:, 128 * c:128 * c + 128], T.cmp[:, 256 * c:256 * c + 128], T.cmp[:, 256 * c + 128:256 * c + 256],
+                 A.add, A.add, "cmp%d" % c, "cs%d" % c)
+        cp(T.offa[:, 0:2], T.cs[:, 127:256:128], "cs0 cs1", "offa0")
+        ts(T.offa[:, 2:4], T.acc[:, 0:2], float(C + SKIP), A.add, "acc0 acc1", "offa2", 0.5, A.mult)
+        cp(T.nval[:, 0:64], T.nxrow[:].indirect(T.offa[:, 0:4]), "nxrow nxpad offa0 offa2", "nval")
+        hold(T.nsc[:], T.nval[:, 8:72], 64, "nval nvpad", "nsc")
+        ts(T.offa[:, 4:8], T.nsc[:, 15:64:16], INV, A.mult, "nsc inv", "offa1")
+        for b in range(4):
+            win = T.th[:, PW * b:PW * b + H0].indirect(T.offa[:])
+            (cp if b < 2 else act)(T.at[:, b:512:4], win, "t%d tz%d offa0 offa1 offa2" % (b, b), "a%d" % b)
+        qa, sa = T["qa%d" % r], T["sa%d" % r]
+        quant(qa[:], sa[:], T.at[:], "a0 a1 a2 a3", "qa%d" % r)
+        lo = LW * (R - 1 - r)
+        send(T.lq[:, lo:lo + LW].bitcast(dt.uint8), qa[:, 8:8 + LW].bitcast(dt.uint8), "qa%d" % r, "ara%d" % r, "loa%d" % r)
+        send(T.ls[:, lo:lo + LW], sa[:, 8:8 + LW], "qa%d" % r, "ara%d" % r, "loa%d" % r)
+
+        tt(T.hh[:, 16:272], T.sg[:].indirect(T.nx16[:]), T.fl[:], A.is_gt, "fl0 fl1 sg0 sg1 nx16", "hh")
+        if r == 0:
+            hold(T.pvs[:], T.pvrow[:], 256, "pvrow", "pvs")
+        else:
+            hold(T.cv[:, 512:768], T.fl[:], 256, "fl0 fl1", "cvf")
+        scan(T.zz[:], T.hh[:, 16:272], T.hh[:, 15:271], A.add, A.add, "hh hhpad", "zz")
+        if r == 0:
+            ts(T.pv16[:], T.pvs[:, 15:256:16], INV, A.mult, "pvs inv", "pv16")
+        act(T.zp[:], T.zz[:].indirect(T.pv16[:]), "zz pv16", "zp")
+        if r == 0:
+            ts(T.pvf[:], T.pvs[:, 15:256:16], INV, A.mult, "pvs inv", "pvf")
+            hold(T.cv[:, 512:768], T.fl[:], 256, "fl0 fl1", "cvf")
+            quant(T.lq[:, R * LW:R * LW + 128], T.ls[:, R * LW:R * LW + 128], T.ht[:], HK + " hpad", "lpad")
+            tt(T.dp0[:], T.pvf[:], T.nxi[:], A.subtract, "pvf nxi", "dp0")
+            tt(T.jn[:], T.jw[:], T.nxi[:], A.subtract, "jw nxi", "jn")
+            ts(T.dpn[:], T.dp0[:], INV, A.mult, "dp0 inv", "dpn")
+            ts(T.cc[:, 0:16], T.jw[:], -1.0, A.mult, "jw", "cc0", float(H0), A.add)
+            ts(T.cc[:, 16:32], T.jw[:], -1.0, A.mult, "jw", "cc1", float(H0 + K), A.add)
+            ts(NW, T.pm[:, 0:1], 15.0, A.not_equal, "pm", "nw0", -BIG, A.mult)
+            ts(T.jq[:], T.jw[:], 0.25, A.add, "jw", "jq")
+            ts(NW, NW, -1.0, A.min, "nw0", "nw")
+            ts(SC, INV, float(K), A.mult, "inv", "sc")
+        tt(T.ta[:], T.cv[:, 527:768:16], T.dpn[:], A.mult, "cvf dpn", "ta")
+        hold(T.cv[:, 0:256], T.zz[:], 256, "zz", "cvz")
+        tt(T.tb[:], T.jn[:], T.ta[:], A.subtract, "jn ta", "tb")
+        if r == 0:
+            ts(RSC, NW, -1.0 / K, A.mult, "nw", "rsc")
+        if r == 1:
+            quant(T.qv[:], T.sv[:], T.vin[:], "vin", "qv")
+        ts(T.nm2[:, 0:1], T.nl[:, 8 * r + 1:8 * r + 2], float(K), A.min, "nl%d" % r, "nm2", 2.0, A.mult)
+        hold(T.cv[:, 256:512], T.zp[:], 256, "zp", "cvp")
+        ts(T.ui[:, 0:32], T.cv[:, 15:512:16], INV, A.mult, "cvz cvp inv", "ui")
+        ts(T.ui[:, 32:64], T.cv[:, 15:512:16], INV, A.mult, "cvz cvp inv nm2", "uc", T.nm2[:, 0:1], A.min)
+        ts(T.kf[:], T.ui[:, 0:32], 1, A.arith_shift_right, "ui", "kf")
+        ts(T.odd[:], T.ui[:], 1, A.bitwise_and, "ui uc", "odd")
+        tt(T.ww[:], T.kf[:], T.cc[:], A.add, "kf cc0 cc1", "ww")
+        tt(T.nsp[:], T.odd[:, 0:16], T.odd[:, 16:32], A.is_equal, "odd", "nsp")
+        tt(T.vw[:], T.odd[:, 32:64], T.ww[:], A.mult, "odd ww", "vw")
+        tt(T.tc[:], T.tb[:], T.nsp[:], A.mult, "tb nsp", "tc")
+        tt(T.td[:], T.vw[:, 0:16], T.vw[:, 16:32], A.add, "vw", "td")
+        tt(T.te[:], T.jq[:], T.tc[:], A.subtract, "jq tc", "te")
+        ts(T.tv[:], T.odd[:, 48:64], NW, A.mult, "odd nw", "tv")
+        tt(T.kk[:], T.td[:], T.te[:], A.add, "td te", "kk")
+
+        before = "lpad" if r == 0 else "land%d" % (r - 1)
+        deps("t", "wq wsc " + before, "PD0 PD1 PD2 PD3 PP")
+        for b in range(4):
+            mm(T.pd[:, 512 * b:512 * b + 128], T.wq[:, 128 * b:128 * b + 128], T.wsc[:, 128 * b:128 * b + 128],
+               T.lq[:, lo:lo + 128], T.ls[:, lo:lo + 128], "wq wsc land%d %s" % (r, before), "PD%d" % b)
+        for b in range(4):
+            o, i = T.ht[:, b:4 * LW:4], T.pd[:, 512 * b:512 * b + LW]
+            if b % 2 == 1:
+                ts(o, i, 0.03125, A.mult, "PD%d" % b, "h%d" % b)
+            else:
+                act(o, i, "PD%d" % b, "h%d" % b, scale=0.03125)
+        qh, sh = T["qh%d" % r], T["sh%d" % r]
+        quant(qh[:], sh[:], T.ht[:], HK + " hpad", "qh")
+        mm(T.pp[:, 0:128], T.qur[:], T.sur[:], qh[:], sh[:], "qur sur qh", "PP")
+        for b in range(4):
+            act(T.th[:, PW * b + H0:PW * b + PW], T.ht[:, b:4 * LW:4], "h%d" % b, "hp%d" % b)
+        ts(T.kr[:], T.kk[:], RSC, A.mult, "kk rsc", "kr")
+        cp(T.kk16[:], T.kk[:], "kk", "kk16")
+        tt(T.base[:], T.kr[:], T.tv[:], A.add, "kr tv", "base")
+        cp(T.pa[:, 0:K], T.pp[:, 0:K], "PP", "pa")
+        tt(T.gt[:, H0:H0 + K], T.pp[:, K:LW], T.pa[:, 0:K], A.is_gt, "PP pa", "g1")
+        tt(T.gt[:, H0 + K:PW], T.pp[:, K:LW], T.pa[:, 0:K], A.is_le, "PP pa", "g2")
+        cp(T.dv[:, 0:128], T.gt[:].indirect(T.kk16[:, 0:8]), "g0 g1 g2 kk16", "dv0")
+        act(T.dv[:, 128:256], T.gt[:].indirect(T.kk16[:, 8:16]), "g0 g1 g2 kk16", "dv1")
+        hold(T.ds[:], T.dv[:], 256, "dv0 dv1", "ds")
+        tt(T.fin[:], T.ds[:, 15:256:16], T.base[:], A.add, "ds base", "fin")
+        ts(T.offx[:], T.fin[:], SC, A.mult, "fin sc", "offx")
+        xs = T["xs%d" % r]
+        for b in range(4):
+            win = T.th[:, PW * b:PW * b + PW].indirect(T.offx[:])
+            (cp if b < 2 else act)(xs[:, b:1024:4], win, "t%d tz%d hp%d offx" % (b, b, b), "x%d" % b)
+
+    act(T.otr[:], T.spec[:].indirect(T.offx[:]), "spec0 spec1 offx", "otr")
+    quant_x(R)
+    qx, sx = T["qx%d" % R], T["sx%d" % R]
+    for h in range(2):
+        mm(T.ps[:, 512 * h:512 * h + 128], T.qv[:], T.sv[:], qx[:, 128 * h:128 * h + 128],
+           sx[:, 128 * h:128 * h + 128], "qv qx%d" % h, "PS%d" % h)
+    for h in range(2):
+        cp(T.ysb[:, 128 * h:128 * h + 128], T.ps[:, 512 * h:512 * h + 128], "PS%d" % h, "y%d" % h)
+    dma("y", T.oc[:], qx[:].bitcast(dt.uint8), "qx0 qx1", "")
+    dma("s", T.ot[:], T.otr[0:128:16, :], "otr", "")
+    dma("s", T.y[:], T.ysb[:], "y0 y1", "")
+    for k in range(4):
+        dma("y" if k < 3 else "s", T.osc[4 * k:4 * k + 4, :], sx[32 * k:32 * k + 4, :], "qx0 qx1", "")
+
+    for sem, cnt in total.items():
+        need("g", ("end", sem, cnt, {}))

@@ -154,7 +154,7 @@ def rank_program(g, core, T, topo):
     deps("y", "uin xin0 xin1", "")
     dma("y", T.wq[:].bitcast(dt.uint8), T.wc[:], "", "wq")
     dma("y", T.wsc[:], T.ws[:], "", "wsc")
-    dma("y", T.vin[:], T.v[:], "", "vin")
+    dma("y", T.vin[:], T.v[:], "land0", "vin")
 
     iota(T.i1[:], [[1, 128]], 0, -1, "i1")
     iota(T.ip[:], [[0, 16]], 0, 1, "ip")
@@ -178,6 +178,8 @@ def rank_program(g, core, T, topo):
     ts(INV, T.pm[:, 0:1], 15.0, A.is_equal, "pm", "inv", 1.0 / BIG, A.max)
     ts(T.thr[:, 0:2], T.jw[:, 0:2], -8.0, A.add, "jw", "thr")
     ts(T.thb[:, 0:2], T.jw[:, 2:4], -7.5, A.add, "jw", "thb")
+    ts(T.ka[:], T.j32[:], PM, A.not_equal, "j32 pmf", "ka")
+    ts(T.kb[:], T.j32[:], PM1, A.is_equal, "j32 pm1", "kb", BIG, A.mult)
 
     for b in range(4):
         act(T.th[:, PW * b + C:PW * b + H0], T.ht[:, 0:16], HK, "tz%d" % b)
@@ -186,23 +188,38 @@ def rank_program(g, core, T, topo):
     act(T.gt[:, 0:H0], T.ht[:, 0:H0], HK, "g0")
 
     cp(T.nx16[:], T.nxi[:], "nxi", "nx16")
-    ts(T.ka[:], T.j32[:], PM, A.not_equal, "j32 pmf", "ka")
-    ts(T.kb[:], T.j32[:], PM1, A.is_equal, "j32 pm1", "kb", BIG, A.mult)
-    act(T.nxrow[:, 0:256], T.jrow[:].indirect(T.nx16[:]), "jrow nx16", "nxrow")
     tt(T.kx[:, 0:32], T.ka[:], T.kb[:], A.max, "ka kb", "kx0")
-    cp(T.pvrow[:].indirect(T.nx16[:]), T.jrow[:], "jrow nx16", "pvrow")
+    act(T.nxrow[:, 0:256], T.jrow[:].indirect(T.nx16[:]), "jrow nx16", "nxrow")
     quant(T.qu[:], T.su[:], T.uin[:], "uin", "qu")
+    ts(NW, T.pm[:, 0:1], 15.0, A.not_equal, "pm", "nw0", -BIG, A.mult)
+    ts(T.jq[:], T.jw[:], 0.25, A.add, "jw", "jq")
     cp(T.qur[:].bitcast(dt.uint32), T.qu[:].bitcast(dt.uint32).indirect(T.uoff[:]), "qu uoff", "qur")
+    act(T.sur[:], T.su[:].indirect(T.uoff[:]), "qu uoff", "sur")
     act(T.kx[:, 32:64], T.kx[:, 0:32], "kx0", "kx1")
     act(T.kx[:, 64:128], T.kx[:, 0:64], "kx1", "kx2")
     act(T.kx[:, 128:256], T.kx[:, 0:128], "kx2", "kx")
-    act(T.sur[:], T.su[:].indirect(T.uoff[:]), "qu uoff", "sur")
 
     def quant_x(r):
         src = T.xin if r == 0 else T["xs%d" % (r - 1)]
         for h in range(2):
             quant(T["qx%d" % r][:, 128 * h:128 * h + 128], T["sx%d" % r][:, 128 * h:128 * h + 128],
                   src[:, 512 * h:512 * h + 512], "xin%d" % h if r == 0 else "x0 x1 x2 x3", "qx%d" % h)
+
+    def unpack(b):
+        act(T.th[:, PW * b:PW * b + C], T.pd[:, 512 * b:512 * b + 256], "PD%d" % b, "t%d" % b)
+
+    def slide_a():
+        tt(T.ta[:], T.cv[:, 527:768:16], T.dpn[:], A.mult, "cvf dpn", "ta")
+
+    def slide_b():
+        tt(T.tb[:], T.jn[:], T.ta[:], A.subtract, "jn ta", "tb")
+
+    def layer(b):
+        o, i = T.ht[:, b:4 * LW:4], T.pd[:, 512 * b:512 * b + LW]
+        if b % 2 == 1:
+            ts(o, i, 0.03125, A.mult, "PD%d" % b, "h%d" % b)
+        else:
+            act(o, i, "PD%d" % b, "h%d" % b, scale=0.03125)
 
     for r in range(R):
         qx, sx = T["qx%d" % r], T["sx%d" % r]
@@ -214,17 +231,23 @@ def rank_program(g, core, T, topo):
         for b in range(4):
             mm(T.pd[:, 512 * b:512 * b + 256], T.qe[:, 128 * b:128 * b + 128], T.se[:, 128 * b:128 * b + 128],
                qx[:], sx[:], "e%d qx0 qx1" % b, "PD%d" % b)
-
-        def unpack(b):
-            act(T.th[:, PW * b:PW * b + C], T.pd[:, 512 * b:512 * b + 256], "PD%d" % b, "t%d" % b)
+        if r == 0:
+            quant(T.lq[:, R * LW:R * LW + 128], T.ls[:, R * LW:R * LW + 128], T.ht[:], HK + " hpad", "lpad")
+            ts(NW, NW, -1.0, A.min, "nw0", "nw")
+        if r == 2:
+            quant(T.qv[:], T.sv[:], T.vin[:], "vin", "qv")
 
         act(T.sg[:, 0:128], T.ps[:, 0:128], "PS0", "sg0", func=F.Sign)
         act(T.sg[:, 128:256], T.pp[:, 0:128], "PP", "sg1", func=F.Sign)
         for h in (1, 0):
             ts(T.fl[:, 128 * h:128 * h + 128], T.ps[:, 512 * h:512 * h + 128], 0.0, A.is_gt, "PS%d" % h, "fl%d" % h)
-        unpack(0)
-        unpack(1)
+        for b in range(3):
+            unpack(b)
+        if r == 0:
+            ts(T.cc[:, 0:16], T.jw[:], -1.0, A.mult, "jw", "cc0", float(H0), A.add)
         tt(T.mt[:], T.fl[:].indirect(T.nx16[:]), T.sg[:], A.is_lt, "fl0 fl1 sg0 sg1 nx16", "mt")
+        if r == 0:
+            ts(T.cc[:, 16:32], T.jw[:], -1.0, A.mult, "jw", "cc1", float(H0 + K), A.add)
         cum = T.cum[:, 256 * r:256 * r + 256]
         ck = "cum%d" % r
         scan(cum, T.mt[:], T.mt[:], A.add, A.max, "mt", ck)
@@ -232,95 +255,99 @@ def rank_program(g, core, T, topo):
         for c in range(2):
             count(T.sgn[:, 256 * c:256 * c + C - SKIP], T.cum[:, 256 * r + SKIP:256 * r + 256], T.thb[:, c:c + 1],
                   T.acc[:, c:c + 1], ck + " thb", "acc%d" % c)
-        unpack(2)
         unpack(3)
+        if r == 0:
+            ts(SC, INV, float(K), A.mult, "inv", "sc")
         for c in range(2):
             ts(T.cmp[:, 256 * c:256 * c + 256], cum, T.thr[:, c:c + 1], A.is_le, ck + " thr", "cmp%d" % c)
         for c in range(2):
             scan(T.cs[:, 128 * c:128 * c + 128], T.cmp[:, 256 * c:256 * c + 128], T.cmp[:, 256 * c + 128:256 * c + 256],
                  A.add, A.add, "cmp%d" % c, "cs%d" % c)
+        hold(T.cv[:, 512:768], T.fl[:], 256, "fl0 fl1", "cvf")
         cp(T.offa[:, 0:2], T.cs[:, 127:256:128], "cs0 cs1", "offa0")
         ts(T.offa[:, 2:4], T.acc[:, 0:2], float(C + SKIP), A.add, "acc0 acc1", "offa2", 0.5, A.mult)
+        if r > 0:
+            slide_a()
+        else:
+            ts(RSC, NW, -1.0 / K, A.mult, "nw", "rsc")
         cp(T.nval[:, 0:64], T.nxrow[:].indirect(T.offa[:, 0:4]), "nxrow nxpad offa0 offa2", "nval")
+        for b in range(4):
+            act(T.at[:, b:256:4], T.th[:, PW * b:PW * b + H0].indirect(T.offa[:, 0:4]),
+                "t%d tz%d offa0 offa2" % (b, b), "a%d" % b)
+        if r > 0:
+            slide_b()
+        else:
+            tt(T.jn[:], T.jw[:], T.nxi[:], A.subtract, "jw nxi", "jn")
         hold(T.nsc[:], T.nval[:, 8:72], 64, "nval nvpad", "nsc")
         ts(T.offa[:, 4:8], T.nsc[:, 15:64:16], INV, A.mult, "nsc inv", "offa1")
         for b in range(4):
-            win = T.th[:, PW * b:PW * b + H0].indirect(T.offa[:])
-            (cp if b < 2 else act)(T.at[:, b:512:4], win, "t%d tz%d offa0 offa1 offa2" % (b, b), "a%d" % b)
+            win = T.th[:, PW * b:PW * b + H0].indirect(T.offa[:, 4:8])
+            (cp if b < 2 else act)(T.at[:, 256 + b:512:4], win, "t%d tz%d offa1" % (b, b), "n%d" % b)
         qa, sa = T["qa%d" % r], T["sa%d" % r]
-        quant(qa[:], sa[:], T.at[:], "a0 a1 a2 a3", "qa%d" % r)
+        quant(qa[:], sa[:], T.at[:], "a0 a1 a2 a3 n0 n1 n2 n3", "qa%d" % r)
         lo = LW * (R - 1 - r)
         send(T.lq[:, lo:lo + LW].bitcast(dt.uint8), qa[:, 8:8 + LW].bitcast(dt.uint8), "qa%d" % r, "ara%d" % r, "loa%d" % r)
         send(T.ls[:, lo:lo + LW], sa[:, 8:8 + LW], "qa%d" % r, "ara%d" % r, "loa%d" % r)
 
+        if r == 0:
+            cp(T.pvrow[:].indirect(T.nx16[:]), T.jrow[:], "jrow nx16", "pvrow")
         tt(T.hh[:, 16:272], T.sg[:].indirect(T.nx16[:]), T.fl[:], A.is_gt, "fl0 fl1 sg0 sg1 nx16", "hh")
         if r == 0:
             hold(T.pvs[:], T.pvrow[:], 256, "pvrow", "pvs")
-        else:
-            hold(T.cv[:, 512:768], T.fl[:], 256, "fl0 fl1", "cvf")
         scan(T.zz[:], T.hh[:, 16:272], T.hh[:, 15:271], A.add, A.add, "hh hhpad", "zz")
         if r == 0:
             ts(T.pv16[:], T.pvs[:, 15:256:16], INV, A.mult, "pvs inv", "pv16")
-        act(T.zp[:], T.zz[:].indirect(T.pv16[:]), "zz pv16", "zp")
-        if r == 0:
             ts(T.pvf[:], T.pvs[:, 15:256:16], INV, A.mult, "pvs inv", "pvf")
-            hold(T.cv[:, 512:768], T.fl[:], 256, "fl0 fl1", "cvf")
-            quant(T.lq[:, R * LW:R * LW + 128], T.ls[:, R * LW:R * LW + 128], T.ht[:], HK + " hpad", "lpad")
-            tt(T.dp0[:], T.pvf[:], T.nxi[:], A.subtract, "pvf nxi", "dp0")
-            tt(T.jn[:], T.jw[:], T.nxi[:], A.subtract, "jw nxi", "jn")
-            ts(T.dpn[:], T.dp0[:], INV, A.mult, "dp0 inv", "dpn")
-            ts(T.cc[:, 0:16], T.jw[:], -1.0, A.mult, "jw", "cc0", float(H0), A.add)
-            ts(T.cc[:, 16:32], T.jw[:], -1.0, A.mult, "jw", "cc1", float(H0 + K), A.add)
-            ts(NW, T.pm[:, 0:1], 15.0, A.not_equal, "pm", "nw0", -BIG, A.mult)
-            ts(T.jq[:], T.jw[:], 0.25, A.add, "jw", "jq")
-            ts(NW, NW, -1.0, A.min, "nw0", "nw")
-            ts(SC, INV, float(K), A.mult, "inv", "sc")
-        tt(T.ta[:], T.cv[:, 527:768:16], T.dpn[:], A.mult, "cvf dpn", "ta")
+        else:
+            ts(T.nm2[:, 0:1], T.nl[:, 8 * r + 1:8 * r + 2], float(K), A.min, "nl%d" % r, "nm2", 2.0, A.mult)
+        act(T.zp[:, 96:256], T.zz[:].indirect(T.pv16[:, 6:16]), "zz pv16", "zp1")
+        cp(T.zp[:, 0:96], T.zz[:].indirect(T.pv16[:, 0:6]), "zz pv16", "zp0")
         hold(T.cv[:, 0:256], T.zz[:], 256, "zz", "cvz")
-        tt(T.tb[:], T.jn[:], T.ta[:], A.subtract, "jn ta", "tb")
         if r == 0:
-            ts(RSC, NW, -1.0 / K, A.mult, "nw", "rsc")
-        if r == 1:
-            quant(T.qv[:], T.sv[:], T.vin[:], "vin", "qv")
-        ts(T.nm2[:, 0:1], T.nl[:, 8 * r + 1:8 * r + 2], float(K), A.min, "nl%d" % r, "nm2", 2.0, A.mult)
-        hold(T.cv[:, 256:512], T.zp[:], 256, "zp", "cvp")
+            tt(T.dp0[:], T.pvf[:], T.nxi[:], A.subtract, "pvf nxi", "dp0")
+        hold(T.cv[:, 256:512], T.zp[:], 256, "zp0 zp1", "cvp")
+        if r == 0:
+            ts(T.dpn[:], T.dp0[:], INV, A.mult, "dp0 inv", "dpn")
+            ts(T.nm2[:, 0:1], T.nl[:, 1:2], float(K), A.min, "nl0", "nm2", 2.0, A.mult)
         ts(T.ui[:, 0:32], T.cv[:, 15:512:16], INV, A.mult, "cvz cvp inv", "ui")
         ts(T.ui[:, 32:64], T.cv[:, 15:512:16], INV, A.mult, "cvz cvp inv nm2", "uc", T.nm2[:, 0:1], A.min)
+        if r == 0:
+            slide_a()
         ts(T.kf[:], T.ui[:, 0:32], 1, A.arith_shift_right, "ui", "kf")
         ts(T.odd[:], T.ui[:], 1, A.bitwise_and, "ui uc", "odd")
+        if r == 0:
+            slide_b()
         tt(T.ww[:], T.kf[:], T.cc[:], A.add, "kf cc0 cc1", "ww")
-        tt(T.nsp[:], T.odd[:, 0:16], T.odd[:, 16:32], A.is_equal, "odd", "nsp")
-        tt(T.vw[:], T.odd[:, 32:64], T.ww[:], A.mult, "odd ww", "vw")
-        tt(T.tc[:], T.tb[:], T.nsp[:], A.mult, "tb nsp", "tc")
-        tt(T.td[:], T.vw[:, 0:16], T.vw[:, 16:32], A.add, "vw", "td")
-        tt(T.te[:], T.jq[:], T.tc[:], A.subtract, "jq tc", "te")
-        ts(T.tv[:], T.odd[:, 48:64], NW, A.mult, "odd nw", "tv")
-        tt(T.kk[:], T.td[:], T.te[:], A.add, "td te", "kk")
 
         before = "lpad" if r == 0 else "land%d" % (r - 1)
         deps("t", "wq wsc " + before, "PD0 PD1 PD2 PD3 PP")
         for b in range(4):
             mm(T.pd[:, 512 * b:512 * b + 128], T.wq[:, 128 * b:128 * b + 128], T.wsc[:, 128 * b:128 * b + 128],
                T.lq[:, lo:lo + 128], T.ls[:, lo:lo + 128], "wq wsc land%d %s" % (r, before), "PD%d" % b)
-        for b in range(4):
-            o, i = T.ht[:, b:4 * LW:4], T.pd[:, 512 * b:512 * b + LW]
-            if b % 2 == 1:
-                ts(o, i, 0.03125, A.mult, "PD%d" % b, "h%d" % b)
-            else:
-                act(o, i, "PD%d" % b, "h%d" % b, scale=0.03125)
+        layer(0)
+        layer(1)
+        tt(T.nsp[:], T.odd[:, 0:16], T.odd[:, 16:32], A.is_equal, "odd", "nsp")
+        layer(2)
+        layer(3)
+        tt(T.vw[:], T.odd[:, 32:64], T.ww[:], A.mult, "odd ww", "vw")
+        tt(T.tc[:], T.tb[:], T.nsp[:], A.mult, "tb nsp", "tc")
         qh, sh = T["qh%d" % r], T["sh%d" % r]
         quant(qh[:], sh[:], T.ht[:], HK + " hpad", "qh")
         mm(T.pp[:, 0:128], T.qur[:], T.sur[:], qh[:], sh[:], "qur sur qh", "PP")
         for b in range(4):
             act(T.th[:, PW * b + H0:PW * b + PW], T.ht[:, b:4 * LW:4], "h%d" % b, "hp%d" % b)
-        ts(T.kr[:], T.kk[:], RSC, A.mult, "kk rsc", "kr")
-        cp(T.kk16[:], T.kk[:], "kk", "kk16")
-        tt(T.base[:], T.kr[:], T.tv[:], A.add, "kr tv", "base")
+        tt(T.td[:], T.vw[:, 0:16], T.vw[:, 16:32], A.add, "vw", "td")
+        tt(T.te[:], T.jq[:], T.tc[:], A.subtract, "jq tc", "te")
+        ts(T.tv[:], T.odd[:, 48:64], NW, A.mult, "odd nw", "tv")
+        tt(T.kk[:], T.td[:], T.te[:], A.add, "td te", "kk")
         cp(T.pa[:, 0:K], T.pp[:, 0:K], "PP", "pa")
+        cp(T.kk16[:], T.kk[:], "kk", "kk16")
         tt(T.gt[:, H0:H0 + K], T.pp[:, K:LW], T.pa[:, 0:K], A.is_gt, "PP pa", "g1")
         tt(T.gt[:, H0 + K:PW], T.pp[:, K:LW], T.pa[:, 0:K], A.is_le, "PP pa", "g2")
-        cp(T.dv[:, 0:128], T.gt[:].indirect(T.kk16[:, 0:8]), "g0 g1 g2 kk16", "dv0")
+        ts(T.kr[:], T.kk[:], RSC, A.mult, "kk rsc", "kr")
         act(T.dv[:, 128:256], T.gt[:].indirect(T.kk16[:, 8:16]), "g0 g1 g2 kk16", "dv1")
+        cp(T.dv[:, 0:128], T.gt[:].indirect(T.kk16[:, 0:8]), "g0 g1 g2 kk16", "dv0")
+        tt(T.base[:], T.kr[:], T.tv[:], A.add, "kr tv", "base")
         hold(T.ds[:], T.dv[:], 256, "dv0 dv1", "ds")
         tt(T.fin[:], T.ds[:, 15:256:16], T.base[:], A.add, "ds base", "fin")
         ts(T.offx[:], T.fin[:], SC, A.mult, "fin sc", "offx")

from concourse.mybir import dt, AluOpType as A, ActivationFunctionType as F

R, C, K = 3, 256, 56
PW = 384
H0 = 272
LW = 2 * K
BIG = float(2 ** 24)
SKIP = 24
X4, U8, BF, F32, I32, U16 = "float8_e4m3fn_x4", "uint8", "bfloat16", "float32", "int32", "uint16"

SCRATCH = {"ps": ("psum", [128, 1024], F32), "pd": ("psum", [128, 2048], F32), "pp": ("psum", [128, 512], F32)}
for _d, _l in (
    (BF, "xin 1024 uin 512 vin 512 ze 528 nl 32 th 1536 at 512 ht 512 j32 32 jrow 256 thr 8 ka 32 kb 32 kx 256 "
         "nxrow 272 pvrow 256 pvs 256 fl 256 sg 256 mt 256 cum 768 cmp 512 cs 256 sgn 512 nval 80 nsc 64 hh 272 "
         "zz 256 zp 256 cv 768 gt 384 dv 256 ds 256 xs0 1024 xs1 1024 xs2 1024"),
    (X4, "wq 512 qu 128 qur 128 qv 128 qe 512 lq 464 qx0 256 qx1 256 qx2 256 qx3 256 qa0 128 qa1 128 qa2 128 "
         "qh0 128 qh1 128 qh2 128"),
    (U8, "wsc 512 su 128 sur 128 sv 128 se 512 ls 464 sx0 256 sx1 256 sx2 256 sx3 256 sa0 128 sa1 128 sa2 128 "
         "sh0 128 sh1 128 sh2 128"),
    (I32, "nxi 16 i1 128 i3 16 ip 16 pm 16 ui 64 odd 64 kf 32"),
    (U16, "uoff 8 nx16 16 pv16 16 offa 8 kk16 16 offx 16"),
    (F32, "spec 384 col 16 jw 16 jq 16 thb 8 pvf 16 dp0 16 acc 8 pa 64 cc 32 jn 16 dpn 16 nm2 8 ww 32 "
          "vw 32 ta 16 tb 16 nsp 16 tc 16 td 16 te 16 kk 16 tv 16 kr 16 base 16 fin 16 otr 256 ysb 256"),
):
    _w = _l.split()
    for _i in range(0, len(_w), 2):
        SCRATCH[_w[_i]] = ("sbuf", [128, int(_w[_i + 1])], _d)

SEMAPHORES = (["cv_", "cs_", "ct_", "cg_"] + ["d%d" % i for i in range(16)]
              + ["%s%d" % (n, r) for n in ("arn", "ara", "lon", "loa") for r in range(R)])


def rank_program(g, core, T, topo):
    rank = T.rank_of(core)
    if rank is None:
        return
    cores = list(T.cores)
    nxt, prv = cores[(rank + 1) % len(cores)], cores[rank - 1]
    rid, pid = topo.addr(nxt)[:2]
    out_mask, n_out, n_in = topo.mask(core, nxt), len(topo.engines(core, nxt)), len(topo.engines(prv, core))

    Q = {"v": g.vector, "s": g.scalar, "t": g.tensor, "g": g, "y": g.sync}
    own = {"v": "cv_", "s": "cs_", "t": "ct_", "g": "cg_"}
    total = {}
    known = {e: {} for e in Q}
    wrote, read = {}, {}
    ndma = [0]

    def need(e, ev):
        sem, cnt, clock = ev[1], ev[2], ev[3]
        if known[e].get(sem, 0) >= cnt:
            return
        Q[e].wait_ge(T.sem[sem], cnt)
        known[e][sem] = cnt
        for k, c in clock.items():
            if known[e].get(k, 0) < c:
                known[e][k] = c

    def deps(e, reads, writes):
        evs = []
        for k in reads.split():
            if k in wrote:
                evs.append(wrote[k])
            if k[0] == "P":
                evs += [x for x in read.get(k, []) if x[0] != e]
        for k in writes.split():
            if k in wrote:
                evs.append(wrote[k])
            evs += read.get(k, [])
        for ev in sorted(evs, key=lambda x: -x[2]):
            need(e, ev)

    def note(ev, reads, writes):
        for k in reads.split():
            read.setdefault(k, []).append(ev)
        for k in writes.split():
            wrote[k] = ev
            read[k] = []

    def op(e, fn, reads, writes):
        deps(e, reads, writes)
        sem = own[e]
        total[sem] = total.get(sem, 0) + 1
        fn().then_inc(T.sem[sem], 1)
        note((e, sem, total[sem], dict(known[e])), reads, writes)

    def dma(e, out, in_, reads, writes):
        deps(e, reads, writes)
        sem = "d%d" % ndma[0]
        ndma[0] += 1
        total[sem] = 16
        Q[e].dma_start(out, in_).then_inc(T.sem[sem], 16)
        note(("dma", sem, 16, dict(known[e])), reads, writes)

    def send(out, in_, reads, rsem, lsem):
        deps("g", reads, "")
        g.remote_dma(out, in_, T.sem[rsem], T.sem[lsem], pid, rid, out_mask)
        total[lsem] = total.get(lsem, 0) + n_out

    V, S, PE = g.vector, g.scalar, g.tensor

    def ts(out, in0, s1, o0, reads, writes, s2=None, o1=None):
        if o1 is None:
            op("v", lambda: V.tensor_scalar(out, in0, s1, None, o0), reads, writes)
        else:
            op("v", lambda: V.tensor_scalar(out, in0, s1, s2, o0, o1), reads, writes)

    def tt(out, a, b, o, reads, writes):
        op("v", lambda: V.tensor_tensor(out, a, b, o), reads, writes)

    def cp(out, in_, reads, writes):
        op("v", lambda: V.tensor_copy(out, in_), reads, writes)

    def scan(out, d0, d1, o0, o1, reads, writes):
        op("v", lambda: V.tensor_tensor_scan(out, d0, d1, 0.0, o0, o1), reads, writes)

    def hold(out, row, n, reads, writes):
        scan(out, T.kx[:, 0:n], row, A.mult, A.add, reads + " kx", writes)

    def quant(q, s, in_, reads, writes):
        op("v", lambda: V.quantize_mx(q, s, in_), reads, writes)

    def act(out, in_, reads, writes, scale=None, func=F.Copy):
        if scale is not None:
            op("s", lambda: S.activation(out, in_, func, scale=scale), reads, writes)
        else:
            op("s", lambda: S.activation(out, in_, func), reads, writes)

    def count(out, in_, bias, acc, reads, writes):
        op("s", lambda: S.activation(out, in_, F.Sign, bias=bias, scale=-1.0, accum_out=acc), reads, writes)

    def mm(out, w, ws, x, xs, reads, writes):
        op("t", lambda: PE.matmul_mx(out, w, ws, x, xs, True, True), reads, writes)

    def iota(out, pat, base, cm, key, small=False):
        if small:
            op("g", lambda: g.iota(out, pat, base, cm, allow_small_or_imprecise_dtypes=True), "", key)
        else:
            op("g", lambda: g.iota(out, pat, base, cm), "", key)

    for r in range(R):
        total["arn%d" % r] = n_in
        total["ara%d" % r] = 2 * n_in
        wrote["nl%d" % r] = ("net", "arn%d" % r, n_in, {})
        wrote["land%d" % r] = ("net", "ara%d" % r, 2 * n_in, {})

    HK = "h0 h1 h2 h3"
    PM, PM1, INV, SC, RSC, NW = [T.col[:, i:i + 1] for i in range(6)]

    dma("s", T.nxi[:], T.nx[:], "", "nxi")
    dma("y", T.uin[:], T.u[:], "", "uin")
    dma("s", T.xin[:, 0:512], T.x[:, 0:512], "", "xin0")
    dma("y", T.xin[:, 512:1024], T.x[:, 512:1024], "", "xin1")
    deps("y", "uin xin0 xin1", "")
    dma("y", T.wq[:].bitcast(dt.uint8), T.wc[:], "", "wq")
    dma("y", T.wsc[:], T.ws[:], "", "wsc")
    dma("y", T.vin[:], T.v[:], "land0", "vin")

    iota(T.i1[:], [[1, 128]], 0, -1, "i1")
    iota(T.ip[:], [[0, 16]], 0, 1, "ip")
    iota(T.i3[:], [[16, 16]], 0, 0, "i3")
    iota(T.jrow[:], [[1, 256]], 0, 0, "jrow", True)
    iota(T.j32[:], [[0, 2], [1, 16]], 0, 0, "j32", True)
    iota(T.spec[:, 0:H0], [[1, H0]], 0, 0, "spec0", True)
    iota(T.spec[:, H0:PW], [[1, 2], [2, K]], C, 0, "spec1", True)

    op("v", lambda: V.memset(T.ze[:], 0.0), "", "ze")
    op("v", lambda: V.memset(T.ht[:], 0.0), "", HK + " hpad")
    op("v", lambda: V.memset(T.nxrow[:, 256:272], float(C)), "", "nxpad")
    ts(T.ze[:, 3:515:4], T.i1[:], 0.0, A.is_equal, "i1", "ze")
    ts(T.pm[:], T.ip[:], 15, A.bitwise_and, "ip", "pm")
    cp(T.uoff[:], T.i3[:, 0:8], "i3", "uoff")
    for b in range(4):
        quant(T.qe[:, 128 * b:128 * b + 128], T.se[:, 128 * b:128 * b + 128], T.ze[:, 3 - b:515 - b], "ze", "e%d" % b)
    tt(T.jw[:], T.pm[:], T.i3[:], A.add, "pm i3", "jw")
    cp(PM, T.pm[:, 0:1], "pm", "pmf")
    ts(PM1, T.pm[:, 0:1], 1.0, A.add, "pm", "pm1")
    ts(INV, T.pm[:, 0:1], 15.0, A.is_equal, "pm", "inv", 1.0 / BIG, A.max)
    ts(T.thr[:, 0:2], T.jw[:, 0:2], -8.0, A.add, "jw", "thr")
    ts(T.thb[:, 0:2], T.jw[:, 2:4], -7.5, A.add, "jw", "thb")
    ts(T.ka[:], T.j32[:], PM, A.not_equal, "j32 pmf", "ka")
    ts(T.kb[:], T.j32[:], PM1, A.is_equal, "j32 pm1", "kb", BIG, A.mult)

    for b in range(4):
        act(T.th[:, PW * b + C:PW * b + H0], T.ht[:, 0:16], HK, "tz%d" % b)
    act(T.nval[:, 64:80], T.ht[:, 0:16], HK, "nvpad")
    act(T.hh[:, 0:16], T.ht[:, 0:16], HK, "hhpad")
    act(T.gt[:, 0:H0], T.ht[:, 0:H0], HK, "g0")

    cp(T.nx16[:], T.nxi[:], "nxi", "nx16")
    tt(T.kx[:, 0:32], T.ka[:], T.kb[:], A.max, "ka kb", "kx0")
    act(T.nxrow[:, 0:256], T.jrow[:].indirect(T.nx16[:]), "jrow nx16", "nxrow")
    quant(T.qu[:], T.su[:], T.uin[:], "uin", "qu")
    ts(NW, T.pm[:, 0:1], 15.0, A.not_equal, "pm", "nw0", -BIG, A.mult)
    ts(T.jq[:], T.jw[:], 0.25, A.add, "jw", "jq")
    cp(T.qur[:].bitcast(dt.uint32), T.qu[:].bitcast(dt.uint32).indirect(T.uoff[:]), "qu uoff", "qur")
    act(T.sur[:], T.su[:].indirect(T.uoff[:]), "qu uoff", "sur")
    act(T.kx[:, 32:64], T.kx[:, 0:32], "kx0", "kx1")
    act(T.kx[:, 64:128], T.kx[:, 0:64], "kx1", "kx2")
    act(T.kx[:, 128:256], T.kx[:, 0:128], "kx2", "kx")

    def quant_x(r):
        src = T.xin if r == 0 else T["xs%d" % (r - 1)]
        for h in range(2):
            quant(T["qx%d" % r][:, 128 * h:128 * h + 128], T["sx%d" % r][:, 128 * h:128 * h + 128],
                  src[:, 512 * h:512 * h + 512], "xin%d" % h if r == 0 else "x0 x1 x2 x3", "qx%d" % h)

    def unpack(b):
        act(T.th[:, PW * b:PW * b + C], T.pd[:, 512 * b:512 * b + 256], "PD%d" % b, "t%d" % b)

    def slide_a():
        tt(T.ta[:], T.cv[:, 527:768:16], T.dpn[:], A.mult, "cvf dpn", "ta")

    def slide_b():
        tt(T.tb[:], T.jn[:], T.ta[:], A.subtract, "jn ta", "tb")

    def layer(b):
        o, i = T.ht[:, b:4 * LW:4], T.pd[:, 512 * b:512 * b + LW]
        if b % 2 == 1:
            ts(o, i, 0.03125, A.mult, "PD%d" % b, "h%d" % b)
        else:
            act(o, i, "PD%d" % b, "h%d" % b, scale=0.03125)

    for r in range(R):
        qx, sx = T["qx%d" % r], T["sx%d" % r]
        quant_x(r)
        for h in range(2):
            mm(T.ps[:, 512 * h:512 * h + 128], T.qur[:], T.sur[:], qx[:, 128 * h:128 * h + 128],
               sx[:, 128 * h:128 * h + 128], "qur sur qx%d" % h, "PS%d" % h)
        mm(T.pp[:, 0:128], T.qur[:], T.sur[:], qx[:, 128:256], sx[:, 128:256], "qur sur qx1", "PP")
        for b in range(4):
            mm(T.pd[:, 512 * b:512 * b + 256], T.qe[:, 128 * b:128 * b + 128], T.se[:, 128 * b:128 * b + 128],
               qx[:], sx[:], "e%d qx0 qx1" % b, "PD%d" % b)
        if r == 0:
            quant(T.lq[:, R * LW:R * LW + 128], T.ls[:, R * LW:R * LW + 128], T.ht[:], HK + " hpad", "lpad")
            ts(NW, NW, -1.0, A.min, "nw0", "nw")
        if r == 2:
            quant(T.qv[:], T.sv[:], T.vin[:], "vin", "qv")

        act(T.sg[:, 0:128], T.ps[:, 0:128], "PS0", "sg0", func=F.Sign)
        act(T.sg[:, 128:256], T.pp[:, 0:128], "PP", "sg1", func=F.Sign)
        for h in (1, 0):
            ts(T.fl[:, 128 * h:128 * h + 128], T.ps[:, 512 * h:512 * h + 128], 0.0, A.is_gt, "PS%d" % h, "fl%d" % h)
        for b in range(3):
            unpack(b)
        if r == 0:
            ts(T.cc[:, 0:16], T.jw[:], -1.0, A.mult, "jw", "cc0", float(H0), A.add)
        tt(T.mt[:], T.fl[:].indirect(T.nx16[:]), T.sg[:], A.is_lt, "fl0 fl1 sg0 sg1 nx16", "mt")
        if r == 0:
            ts(T.cc[:, 16:32], T.jw[:], -1.0, A.mult, "jw", "cc1", float(H0 + K), A.add)
        cum = T.cum[:, 256 * r:256 * r + 256]
        ck = "cum%d" % r
        scan(cum, T.mt[:], T.mt[:], A.add, A.max, "mt", ck)
        send(T.nl[:, 8 * r:8 * r + 2], T.cum[:, 256 * r + 254:256 * r + 256], ck, "arn%d" % r, "lon%d" % r)
        for c in range(2):
            count(T.sgn[:, 256 * c:256 * c + C - SKIP], T.cum[:, 256 * r + SKIP:256 * r + 256], T.thb[:, c:c + 1],
                  T.acc[:, c:c + 1], ck + " thb", "acc%d" % c)
        unpack(3)
        if r == 0:
            ts(SC, INV, float(K), A.mult, "inv", "sc")
        for c in range(2):
            ts(T.cmp[:, 256 * c:256 * c + 256], cum, T.thr[:, c:c + 1], A.is_le, ck + " thr", "cmp%d" % c)
        for c in range(2):
            scan(T.cs[:, 128 * c:128 * c + 128], T.cmp[:, 256 * c:256 * c + 128], T.cmp[:, 256 * c + 128:256 * c + 256],
                 A.add, A.add, "cmp%d" % c, "cs%d" % c)
        hold(T.cv[:, 512:768], T.fl[:], 256, "fl0 fl1", "cvf")
        cp(T.offa[:, 0:2], T.cs[:, 127:256:128], "cs0 cs1", "offa0")
        ts(T.offa[:, 2:4], T.acc[:, 0:2], float(C + SKIP), A.add, "acc0 acc1", "offa2", 0.5, A.mult)
        if r > 0:
            slide_a()
        else:
            ts(RSC, NW, -1.0 / K, A.mult, "nw", "rsc")
        cp(T.nval[:, 0:64], T.nxrow[:].indirect(T.offa[:, 0:4]), "nxrow nxpad offa0 offa2", "nval")
        for b in range(4):
            act(T.at[:, b:256:4], T.th[:, PW * b:PW * b + H0].indirect(T.offa[:, 0:4]),
                "t%d tz%d offa0 offa2" % (b, b), "a%d" % b)
        if r > 0:
            slide_b()
        else:
            tt(T.jn[:], T.jw[:], T.nxi[:], A.subtract, "jw nxi", "jn")
        hold(T.nsc[:], T.nval[:, 8:72], 64, "nval nvpad", "nsc")
        ts(T.offa[:, 4:8], T.nsc[:, 15:64:16], INV, A.mult, "nsc inv", "offa1")
        for b in range(4):
            win = T.th[:, PW * b:PW * b + H0].indirect(T.offa[:, 4:8])
            (cp if b < 2 else act)(T.at[:, 256 + b:512:4], win, "t%d tz%d offa1" % (b, b), "n%d" % b)
        qa, sa = T["qa%d" % r], T["sa%d" % r]
        quant(qa[:], sa[:], T.at[:], "a0 a1 a2 a3 n0 n1 n2 n3", "qa%d" % r)
        lo = LW * (R - 1 - r)
        send(T.lq[:, lo:lo + LW].bitcast(dt.uint8), qa[:, 8:8 + LW].bitcast(dt.uint8), "qa%d" % r, "ara%d" % r, "loa%d" % r)
        send(T.ls[:, lo:lo + LW], sa[:, 8:8 + LW], "qa%d" % r, "ara%d" % r, "loa%d" % r)

        if r == 0:
            cp(T.pvrow[:].indirect(T.nx16[:]), T.jrow[:], "jrow nx16", "pvrow")
        tt(T.hh[:, 16:272], T.sg[:].indirect(T.nx16[:]), T.fl[:], A.is_gt, "fl0 fl1 sg0 sg1 nx16", "hh")
        if r == 0:
            hold(T.pvs[:], T.pvrow[:], 256, "pvrow", "pvs")
        scan(T.zz[:], T.hh[:, 16:272], T.hh[:, 15:271], A.add, A.add, "hh hhpad", "zz")
        if r == 0:
            ts(T.pv16[:], T.pvs[:, 15:256:16], INV, A.mult, "pvs inv", "pv16")
            ts(T.pvf[:], T.pvs[:, 15:256:16], INV, A.mult, "pvs inv", "pvf")
        else:
            ts(T.nm2[:, 0:1], T.nl[:, 8 * r + 1:8 * r + 2], float(K), A.min, "nl%d" % r, "nm2", 2.0, A.mult)
        act(T.zp[:, 96:256], T.zz[:].indirect(T.pv16[:, 6:16]), "zz pv16", "zp1")
        cp(T.zp[:, 0:96], T.zz[:].indirect(T.pv16[:, 0:6]), "zz pv16", "zp0")
        hold(T.cv[:, 0:256], T.zz[:], 256, "zz", "cvz")
        if r == 0:
            tt(T.dp0[:], T.pvf[:], T.nxi[:], A.subtract, "pvf nxi", "dp0")
        hold(T.cv[:, 256:512], T.zp[:], 256, "zp0 zp1", "cvp")
        if r == 0:
            ts(T.dpn[:], T.dp0[:], INV, A.mult, "dp0 inv", "dpn")
            ts(T.nm2[:, 0:1], T.nl[:, 1:2], float(K), A.min, "nl0", "nm2", 2.0, A.mult)
        ts(T.ui[:, 0:32], T.cv[:, 15:512:16], INV, A.mult, "cvz cvp inv", "ui")
        ts(T.ui[:, 32:64], T.cv[:, 15:512:16], INV, A.mult, "cvz cvp inv nm2", "uc", T.nm2[:, 0:1], A.min)
        if r == 0:
            slide_a()
        ts(T.kf[:], T.ui[:, 0:32], 1, A.arith_shift_right, "ui", "kf")
        ts(T.odd[:], T.ui[:], 1, A.bitwise_and, "ui uc", "odd")
        if r == 0:
            slide_b()
        tt(T.ww[:], T.kf[:], T.cc[:], A.add, "kf cc0 cc1", "ww")

        before = "lpad" if r == 0 else "land%d" % (r - 1)
        deps("t", "wq wsc " + before, "PD0 PD1 PD2 PD3 PP")
        for b in range(4):
            mm(T.pd[:, 512 * b:512 * b + 128], T.wq[:, 128 * b:128 * b + 128], T.wsc[:, 128 * b:128 * b + 128],
               T.lq[:, lo:lo + 128], T.ls[:, lo:lo + 128], "wq wsc land%d %s" % (r, before), "PD%d" % b)
        layer(0)
        layer(1)
        tt(T.nsp[:], T.odd[:, 0:16], T.odd[:, 16:32], A.is_equal, "odd", "nsp")
        layer(2)
        layer(3)
        tt(T.vw[:], T.odd[:, 32:64], T.ww[:], A.mult, "odd ww", "vw")
        tt(T.tc[:], T.tb[:], T.nsp[:], A.mult, "tb nsp", "tc")
        qh, sh = T["qh%d" % r], T["sh%d" % r]
        quant(qh[:], sh[:], T.ht[:], HK + " hpad", "qh")
        mm(T.pp[:, 0:128], T.qur[:], T.sur[:], qh[:], sh[:], "qur sur qh", "PP")
        for b in range(4):
            act(T.th[:, PW * b + H0:PW * b + PW], T.ht[:, b:4 * LW:4], "h%d" % b, "hp%d" % b)
        tt(T.td[:], T.vw[:, 0:16], T.vw[:, 16:32], A.add, "vw", "td")
        tt(T.te[:], T.jq[:], T.tc[:], A.subtract, "jq tc", "te")
        ts(T.tv[:], T.odd[:, 48:64], NW, A.mult, "odd nw", "tv")
        tt(T.kk[:], T.td[:], T.te[:], A.add, "td te", "kk")
        cp(T.pa[:, 0:K], T.pp[:, 0:K], "PP", "pa")
        cp(T.kk16[:], T.kk[:], "kk", "kk16")
        tt(T.gt[:, H0:H0 + K], T.pp[:, K:LW], T.pa[:, 0:K], A.is_gt, "PP pa", "g1")
        tt(T.gt[:, H0 + K:PW], T.pp[:, K:LW], T.pa[:, 0:K], A.is_le, "PP pa", "g2")
        ts(T.kr[:], T.kk[:], RSC, A.mult, "kk rsc", "kr")
        act(T.dv[:, 128:256], T.gt[:].indirect(T.kk16[:, 8:16]), "g0 g1 g2 kk16", "dv1")
        cp(T.dv[:, 0:128], T.gt[:].indirect(T.kk16[:, 0:8]), "g0 g1 g2 kk16", "dv0")
        tt(T.base[:], T.kr[:], T.tv[:], A.add, "kr tv", "base")
        hold(T.ds[:], T.dv[:], 256, "dv0 dv1", "ds")
        tt(T.fin[:], T.ds[:, 15:256:16], T.base[:], A.add, "ds base", "fin")
        ts(T.offx[:], T.fin[:], SC, A.mult, "fin sc", "offx")
        xs = T["xs%d" % r]
        for b in range(4):
            win = T.th[:, PW * b:PW * b + PW].indirect(T.offx[:])
            (cp if b < 2 else act)(xs[:, b:1024:4], win, "t%d tz%d hp%d offx" % (b, b, b), "x%d" % b)

    act(T.otr[:], T.spec[:].indirect(T.offx[:]), "spec0 spec1 offx", "otr")
    quant_x(R)
    qx, sx = T["qx%d" % R], T["sx%d" % R]
    for h in range(2):
        mm(T.ps[:, 512 * h:512 * h + 128], T.qv[:], T.sv[:], qx[:, 128 * h:128 * h + 128],
           sx[:, 128 * h:128 * h + 128], "qv qx%d" % h, "PS%d" % h)
    for h in range(2):
        cp(T.ysb[:, 128 * h:128 * h + 128], T.ps[:, 512 * h:512 * h + 128], "PS%d" % h, "y%d" % h)
    dma("y", T.oc[:], qx[:].bitcast(dt.uint8), "qx0 qx1", "")
    dma("s", T.ot[:], T.otr[0:128:16, :], "otr", "")
    dma("s", T.y[:], T.ysb[:], "y0 y1", "")
    for k in range(4):
        dma("y" if k < 3 else "s", T.osc[4 * k:4 * k + 4, :], sx[32 * k:32 * k + 4, :], "qx0 qx1", "")

    for sem, cnt in total.items():
        need("g", ("end", sem, cnt, {}))
